import numpy as np
import ml_dtypes


def mxq(x, axis, fmt="e4m3"):
    dtype, down = {"e4m3": (ml_dtypes.float8_e4m3fn, 7), "e5m2": (ml_dtypes.float8_e5m2, 14)}[fmt]
    v = np.moveaxis(np.asarray(x, np.float32).astype(ml_dtypes.bfloat16).astype(np.float64), axis, -1)
    blocks = v.reshape(v.shape[:-1] + (-1, 32))
    amax = np.abs(blocks).max(-1, keepdims=True)
    byte = np.maximum(np.where(amax > 0, np.frexp(amax)[1] - 1 + 127, 0) - down, 1)
    scale = np.exp2(byte - 127.0)
    codes = (blocks / scale).astype(np.float32).astype(dtype).astype(np.float64)
    return np.moveaxis((codes * scale).reshape(v.shape), -1, axis)


WIDE = False


def mx_kscale(k):
    if not WIDE:
        return np.ones(k)
    levels = np.array([10, -10, 5, -5, 0])
    if k % 512:
        return np.exp2(np.random.permutation(np.resize(levels, k // 32))).repeat(32)
    a = np.empty((k // 512, 16))
    for p in range(k // 512):
        a[p, :8] = np.random.permutation(np.resize(levels, 8))
        for g in range(8):
            far = levels[np.abs(levels - a[p, g]) >= 10]
            a[p, g + 8] = far[np.random.randint(len(far))]
    return np.exp2(a.ravel()).repeat(32)


def f64(x):
    return np.asarray(x).astype(np.float64)


def striped8(idx):
    return np.concatenate([v.reshape(-1, 16).T for v in idx]).astype(np.uint16)


def unstriped8(offs):
    return np.stack([offs[16 * g:16 * g + 16].T.reshape(-1) for g in range(8)]).astype(np.int64)


E2M1 = np.array([0.0, 0.5, 1.0, 1.5, 2.0, 3.0, 4.0, 6.0, -0.0, -0.5, -1.0, -1.5, -2.0, -3.0, -4.0, -6.0])


def pack_weight(w, fmt):
    k, n = w.shape
    w = f64(np.asarray(w, np.float32).astype(ml_dtypes.bfloat16)).reshape(k // 32, 32, n)
    amax = np.abs(w).max(1)
    if fmt == "e4m3":
        byte = np.frexp(amax)[1] - 1 + 127 - 7
    else:
        mant, ex = np.frexp(amax / 6.0)
        byte = np.where(mant > 0.5, ex, ex - 1) + 127
    byte = np.clip(np.where(amax > 0, byte, 1), 1, 254)
    scaled = (w * np.exp2(127.0 - byte)[:, None, :]).reshape(k, n).astype(np.float32)
    by_word = np.ascontiguousarray(scaled.reshape(k // 512, 128, 4, n).transpose(0, 1, 3, 2))
    if fmt == "e4m3":
        words = by_word.astype(ml_dtypes.float8_e4m3fn).view(np.uint8)
    else:
        c = by_word.astype(ml_dtypes.float4_e2m1fn).view(np.uint8) & 0xF
        words = (c[..., 0::2] | (c[..., 1::2] << 4)).reshape(k // 512, 128, 2 * n)
    return np.ascontiguousarray(words), np.ascontiguousarray(byte.astype(np.uint8).reshape(k // 512, 16, n))


def unpack_weight(words, scales, fmt):
    g, _, n = scales.shape
    words = np.ascontiguousarray(words).reshape(g, 128, n, -1)
    if fmt == "e4m3":
        vals = words.view(ml_dtypes.float8_e4m3fn).astype(np.float64)
    else:
        nib = np.empty((g, 128, n, 4), np.uint8)
        nib[..., 0::2] = words & 0xF
        nib[..., 1::2] = words >> 4
        vals = E2M1[nib]
    vals = vals * np.repeat(np.exp2(scales.astype(np.float64) - 127.0), 8, axis=1)[..., None]
    return vals.transpose(0, 1, 3, 2).reshape(g * 512, n)


def gelu(v):
    return 0.5 * v * (1.0 + np.tanh(np.sqrt(2.0 / np.pi) * (v + 0.044715 * v**3)))


K, M, T, S = 1536, 256, 1024, 512


def setup_inputs():
    n = np.random.standard_normal
    s = mx_kscale(K)[:, None]
    w = n((K, M)) / np.sqrt(K) / s
    w4 = pack_weight(w, "e2m1")
    rest = w - unpack_weight(*w4, "e2m1")
    p_r8 = pack_weight(rest, "e4m3")
    return {
        "xT": (n((K, T)) * s).astype(np.float32),
        "w4_words": w4[0],
        "w4_scales": w4[1],
        "r8_words": p_r8[0],
        "r8_scales": p_r8[1],
        "wgt": np.repeat(np.random.uniform(0.5, 2.0, (8, S)), 16, axis=0).astype(np.float32),
        "b": (0.3 * n(256)).astype(np.float32),
        "wgo": np.repeat(np.random.uniform(0.5, 2.0, (8, S)), 16, axis=0).astype(np.float32),
        "offs": striped8(np.stack([np.random.permutation(T)[:S] for _ in range(8)])),
        "offs2": striped8(np.stack([np.random.permutation(T)[:S] for _ in range(8)])),
    }


def reference(xT, w4_words, w4_scales, r8_words, r8_scales, wgt, b, wgo, offs, offs2):
    idx = unstriped8(offs)
    group = np.arange(K) % 512 // 64
    xg = f64(wgt)[np.arange(K) // 4 % 128] * f64(xT)[np.arange(K)[:, None], idx[group]]
    xT_ = mxq(xg, 0, "e4m3")
    w4_ = unpack_weight(w4_words, w4_scales, "e2m1")
    r8_ = unpack_weight(r8_words, r8_scales, "e4m3")
    y = w4_.T @ xT_ + r8_.T @ xT_
    place = unstriped8(offs2)[np.arange(M) % 128 // 16]
    out = np.zeros((M, T))
    out[np.arange(M)[:, None], place] = f64(wgo)[np.arange(M) % 128] * (gelu(y + f64(b)[:, None]))
    return out

@@ -1,0 +1,192 @@
+from contextlib import ExitStack
+
+import concourse.mybir as mybir
+
+K, M, T, S = 1536, 256, 1024, 512
+
+F32 = mybir.dt.float32
+BF16 = mybir.dt.bfloat16
+I32 = mybir.dt.int32
+U32 = mybir.dt.uint32
+U16 = mybir.dt.uint16
+U8 = mybir.dt.uint8
+FP8X4 = mybir.dt.float8_e4m3fn_x4
+FP4X4 = mybir.dt.float4_e2m1fn_x4
+MULT = mybir.AluOpType.mult
+GELU = mybir.ActivationFunctionType.Gelu_apprx_tanh
+
+P = 128
+PASSES = K // 512
+HALF = S // 2
+LCOLS = HALF // 16
+NB = 128
+
+FLOPS = 2 * 2 * K * M * S
+
+
+def tile_list_hboth_gelu_kernel(tc, xT, w4_words, w4_scales, r8_words, r8_scales, wgt, b, wgo, offs, offs2, out):
+    nc = tc.nc
+    with ExitStack() as ctx:
+        keep = ctx.enter_context(tc.tile_pool(name="keep", bufs=1))
+        psum = ctx.enter_context(tc.psum_pool(name="psum", bufs=1))
+
+        offs_sb = keep.tile([P, S // 16], U16, name="offs_sb")
+        offs2_sb = keep.tile([P, S // 16], U16, name="offs2_sb")
+        x = [keep.tile([P, T], F32, name="x%d" % i) for i in range(4 * PASSES)]
+        wgt_sb = [keep.tile([P, HALF], F32, name="wgt%d" % s) for s in range(2)]
+        wgo_sb = keep.tile([P, S], F32, name="wgo_sb")
+        b_sb = keep.tile([P, 2], F32, name="b_sb")
+        w4 = keep.tile([P, PASSES, 2 * M], U8, name="w4", align_bytes=64)
+        r8 = keep.tile([P, PASSES, 4 * M], U8, name="r8", align_bytes=64)
+        ws = keep.tile([P, 2, PASSES, M], U8, name="ws", align_bytes=64)
+        win = [keep.tile([P, T], F32, name="win%d" % m) for m in range(2)]
+        warm = keep.tile([P, 1], F32, name="warm")
+
+        nc.sync.dma_start(offs_sb[:], offs)
+        x_view = xT.rearrange("(a p i) t -> a i p t", p=P, i=4)
+
+        def load_x(i):
+            nc.sync.dma_start(x[i][:], x_view[i // 4, i % 4])
+
+        load_x(0)
+        for s in range(2):
+            nc.scalar.dma_start(wgt_sb[s][:], wgt[:, s * HALF : (s + 1) * HALF])
+
+        nc.vector.memset(ws[:].rearrange("p f a m -> p (f a m)").bitcast(I32), 0)
+        for f, scales in enumerate((w4_scales, r8_scales)):
+            for q in range(4):
+                nc.gpsimd.dma_start(
+                    ws[32 * q : 32 * q + 4, f, :, :].bitcast(I32),
+                    scales[:, 4 * q : 4 * q + 4, :].rearrange("a q m -> q a m").bitcast(I32),
+                )
+        with nc.allow_non_contiguous_dma(reason="one bias value a partition"):
+            nc.gpsimd.dma_start(b_sb[:], b.rearrange("(m p) -> p m", p=P))
+        nc.vector.memset(warm[:], 0.0)
+        nc.scalar.activation(warm[:], warm[:], GELU)
+        for m in range(2):
+            nc.vector.memset(win[m][:], 0.0)
+
+        for i in range(1, 10):
+            load_x(i)
+        nc.sync.dma_start(w4[:].bitcast(I32), w4_words.rearrange("a p b -> p a b").bitcast(I32))
+        load_x(10)
+        load_x(11)
+        nc.sync.dma_start(r8[:].bitcast(I32), r8_words.rearrange("a p n i -> p a (n i)").bitcast(I32))
+        nc.sync.dma_start(offs2_sb[:], offs2)
+        nc.sync.dma_start(wgo_sb[:], wgo)
+
+        g4, grouped, codes, scales_x = {}, {}, {}, {}
+        for a in range(PASSES):
+            for s in range(2):
+                k = "_%d%d" % (a, s)
+                g4[a, s] = keep.tile([P, 4, HALF], F32, name="g4" + k)
+                grouped[a, s] = keep.tile([P, HALF, 4], BF16, name="gr" + k, align_bytes=64)
+                codes[a, s] = keep.tile([P, HALF], U32, name="co" + k, align_bytes=64)
+                scales_x[a, s] = keep.tile([P, HALF], U8, name="sc" + k, align_bytes=64)
+        acc = {}
+        for m in range(2):
+            for s in range(2):
+                for c in range(2):
+                    acc[m, s, c] = psum.tile([P, 512], F32, name="acc%d%d%d" % (m, s, c))
+        gel = {}
+        for m in range(2):
+            for s in range(2):
+                gel[m, s] = keep.tile([P, HALF], F32, name="gel%d%d" % (m, s))
+
+        def gather(i, s):
+            nc.vector.tensor_tensor(
+                g4[i // 4, s][:, i % 4, :],
+                x[i][:].indirect(offs_sb[:, s * LCOLS : (s + 1) * LCOLS]),
+                wgt_sb[s][:],
+                MULT,
+            )
+
+        def interleave(eng, a, s):
+            eng(grouped[a, s][:], g4[a, s][:].rearrange("p t n -> p n t"))
+
+        def quantize(a, s):
+            nc.vector.quantize_mx(
+                out=codes[a, s][:].bitcast(FP8X4),
+                scales=scales_x[a, s][:],
+                in_=grouped[a, s][:].rearrange("p n t -> p (n t)"),
+            )
+
+        def multiply(a, s):
+            for m in range(2):
+                for c in range(2):
+                    cols = slice(c * NB, (c + 1) * NB)
+                    for f in range(2):
+                        if f == 0:
+                            w = w4[:, a, 256 * m : 256 * m + 256].bitcast(FP4X4)
+                        else:
+                            w = r8[:, a, 512 * m : 512 * m + 512].bitcast(FP8X4)
+                        nc.tensor.matmul_mx(
+                            out=acc[m, s, c][:, 0:NB],
+                            lhsT=w,
+                            lhsT_scale=ws[:, f, a, 128 * m : 128 * m + 128],
+                            rhs=codes[a, s][:, cols].bitcast(FP8X4),
+                            rhs_scale=scales_x[a, s][:, cols],
+                            start=(a == 0 and f == 0),
+                            stop=(a == PASSES - 1 and f == 1),
+                        )
+
+        def gelu(m, s):
+            for c in range(2):
+                nc.scalar.activation(
+                    gel[m, s][:, c * NB : (c + 1) * NB], acc[m, s, c][:, 0:NB], GELU, bias=b_sb[:, m : m + 1]
+                )
+
+        def scatter(m, s):
+            nc.vector.tensor_tensor(
+                win[m][:].indirect(offs2_sb[:, s * LCOLS : (s + 1) * LCOLS]),
+                gel[m, s][:],
+                wgo_sb[:, s * HALF : (s + 1) * HALF],
+                MULT,
+            )
+
+        for i in range(4):
+            gather(i, 0)
+            gather(i, 1)
+        interleave(nc.scalar.copy, 0, 0)
+        interleave(nc.scalar.copy, 0, 1)
+        for i in range(4, 6):
+            gather(i, 0)
+            gather(i, 1)
+        quantize(0, 0)
+        gather(6, 0)
+        gather(6, 1)
+        quantize(0, 1)
+        multiply(0, 0)
+        multiply(0, 1)
+        gather(7, 0)
+        gather(7, 1)
+        interleave(nc.scalar.copy, 1, 0)
+        interleave(nc.scalar.copy, 1, 1)
+        gather(8, 0)
+        gather(9, 0)
+        gather(8, 1)
+        quantize(1, 0)
+        gather(10, 0)
+        quantize(1, 1)
+        multiply(1, 0)
+        multiply(1, 1)
+        gather(11, 0)
+        interleave(nc.scalar.copy, 2, 0)
+        gather(9, 1)
+        gather(10, 1)
+        quantize(2, 0)
+        multiply(2, 0)
+        gather(11, 1)
+        gelu(0, 0)
+        interleave(nc.vector.tensor_copy, 2, 1)
+        gelu(1, 0)
+        scatter(0, 0)
+        quantize(2, 1)
+        multiply(2, 1)
+        gelu(0, 1)
+        gelu(1, 1)
+        scatter(1, 0)
+        scatter(0, 1)
+        nc.sync.dma_start(out[0:P, :], win[0][:])
+        scatter(1, 1)
+        nc.sync.dma_start(out[P : 2 * P, :], win[1][:])

@@ -49,8 +49,8 @@ def tile_list_hboth_gelu_kernel(tc, xT, w4_words, w4_scales, r8_words, r8_scales
             nc.sync.dma_start(x[i][:], x_view[i // 4, i % 4])
 
         load_x(0)
-        for s in range(2):
-            nc.scalar.dma_start(wgt_sb[s][:], wgt[:, s * HALF : (s + 1) * HALF])
+        nc.scalar.dma_start(wgt_sb[0][:], wgt[:, 0:HALF])
+        nc.sync.dma_start(wgt_sb[1][:], wgt[:, HALF:S])
 
         nc.vector.memset(ws[:].rearrange("p f a m -> p (f a m)").bitcast(I32), 0)
         for f, scales in enumerate((w4_scales, r8_scales)):
@@ -59,8 +59,6 @@ def tile_list_hboth_gelu_kernel(tc, xT, w4_words, w4_scales, r8_words, r8_scales
                     ws[32 * q : 32 * q + 4, f, :, :].bitcast(I32),
                     scales[:, 4 * q : 4 * q + 4, :].rearrange("a q m -> q a m").bitcast(I32),
                 )
-        with nc.allow_non_contiguous_dma(reason="one bias value a partition"):
-            nc.gpsimd.dma_start(b_sb[:], b.rearrange("(m p) -> p m", p=P))
         nc.vector.memset(warm[:], 0.0)
         nc.scalar.activation(warm[:], warm[:], GELU)
         for m in range(2):
@@ -71,18 +69,21 @@ def tile_list_hboth_gelu_kernel(tc, xT, w4_words, w4_scales, r8_words, r8_scales
         nc.sync.dma_start(w4[:].bitcast(I32), w4_words.rearrange("a p b -> p a b").bitcast(I32))
         load_x(10)
         load_x(11)
-        nc.sync.dma_start(r8[:].bitcast(I32), r8_words.rearrange("a p n i -> p a (n i)").bitcast(I32))
+        r8_view = r8_words.rearrange("a p n i -> p a (n i)").bitcast(I32)
+        nc.sync.dma_start(r8[:].bitcast(I32), r8_view)
+        with nc.allow_non_contiguous_dma(reason="one bias value a partition"):
+            nc.sync.dma_start(b_sb[:], b.rearrange("(m p) -> p m", p=P))
         nc.sync.dma_start(offs2_sb[:], offs2)
         nc.sync.dma_start(wgo_sb[:], wgo)
 
         g4, grouped, codes, scales_x = {}, {}, {}, {}
         for a in range(PASSES):
+            grouped[a] = keep.tile([P, S, 4], BF16, name="gr%d" % a, align_bytes=64)
+            codes[a] = keep.tile([P, S], U32, name="co%d" % a, align_bytes=64)
+            scales_x[a] = keep.tile([P, S], U8, name="sc%d" % a, align_bytes=64)
             for s in range(2):
                 k = "_%d%d" % (a, s)
                 g4[a, s] = keep.tile([P, 4, HALF], F32, name="g4" + k)
-                grouped[a, s] = keep.tile([P, HALF, 4], BF16, name="gr" + k, align_bytes=64)
-                codes[a, s] = keep.tile([P, HALF], U32, name="co" + k, align_bytes=64)
-                scales_x[a, s] = keep.tile([P, HALF], U8, name="sc" + k, align_bytes=64)
         acc = {}
         for m in range(2):
             for s in range(2):
@@ -101,21 +102,24 @@ def tile_list_hboth_gelu_kernel(tc, xT, w4_words, w4_scales, r8_words, r8_scales
                 MULT,
             )
 
-        def interleave(eng, a, s):
-            eng(grouped[a, s][:], g4[a, s][:].rearrange("p t n -> p n t"))
-
-        def quantize(a, s):
-            nc.vector.quantize_mx(
-                out=codes[a, s][:].bitcast(FP8X4),
-                scales=scales_x[a, s][:],
-                in_=grouped[a, s][:].rearrange("p n t -> p (n t)"),
+        def interleave(eng, a, s, lo=0, hi=HALF):
+            eng(
+                grouped[a][:, s * HALF + lo : s * HALF + hi, :],
+                g4[a, s][:, :, lo:hi].rearrange("p t n -> p n t"),
             )
 
-        def multiply(a, s):
+        def quantize(a, lo, hi):
+            nc.vector.quantize_mx(
+                out=codes[a][:, lo:hi].bitcast(FP8X4),
+                scales=scales_x[a][:, lo:hi],
+                in_=grouped[a][:, lo:hi, :].rearrange("p n t -> p (n t)"),
+            )
+
+        def multiply(a, s, formats=(0, 1)):
             for m in range(2):
                 for c in range(2):
-                    cols = slice(c * NB, (c + 1) * NB)
-                    for f in range(2):
+                    cols = slice(s * HALF + c * NB, s * HALF + (c + 1) * NB)
+                    for f in formats:
                         if f == 0:
                             w = w4[:, a, 256 * m : 256 * m + 256].bitcast(FP4X4)
                         else:
@@ -124,8 +128,8 @@ def tile_list_hboth_gelu_kernel(tc, xT, w4_words, w4_scales, r8_words, r8_scales
                             out=acc[m, s, c][:, 0:NB],
                             lhsT=w,
                             lhsT_scale=ws[:, f, a, 128 * m : 128 * m + 128],
-                            rhs=codes[a, s][:, cols].bitcast(FP8X4),
-                            rhs_scale=scales_x[a, s][:, cols],
+                            rhs=codes[a][:, cols].bitcast(FP8X4),
+                            rhs_scale=scales_x[a][:, cols],
                             start=(a == 0 and f == 0),
                             stop=(a == PASSES - 1 and f == 1),
                         )
@@ -144,44 +148,46 @@ def tile_list_hboth_gelu_kernel(tc, xT, w4_words, w4_scales, r8_words, r8_scales
                 MULT,
             )
 
+        scopy, vcopy = nc.scalar.copy, nc.vector.tensor_copy
         for i in range(4):
             gather(i, 0)
             gather(i, 1)
-        interleave(nc.scalar.copy, 0, 0)
-        interleave(nc.scalar.copy, 0, 1)
-        for i in range(4, 6):
+        interleave(scopy, 0, 0)
+        interleave(scopy, 0, 1)
+        for i in range(4, 7):
             gather(i, 0)
             gather(i, 1)
-        quantize(0, 0)
-        gather(6, 0)
-        gather(6, 1)
-        quantize(0, 1)
-        multiply(0, 0)
-        multiply(0, 1)
+        quantize(0, 0, S)
+        multiply(0, 0, (0,))
+        multiply(0, 1, (0,))
         gather(7, 0)
         gather(7, 1)
-        interleave(nc.scalar.copy, 1, 0)
-        interleave(nc.scalar.copy, 1, 1)
+        interleave(scopy, 1, 0)
+        interleave(scopy, 1, 1)
         gather(8, 0)
-        gather(9, 0)
         gather(8, 1)
-        quantize(1, 0)
+        gather(9, 0)
         gather(10, 0)
-        quantize(1, 1)
-        multiply(1, 0)
-        multiply(1, 1)
+        quantize(1, 0, S)
+        multiply(1, 0, (0,))
+        multiply(1, 1, (0,))
+        multiply(0, 0, (1,))
+        multiply(1, 0, (1,))
         gather(11, 0)
-        interleave(nc.scalar.copy, 2, 0)
+        interleave(scopy, 2, 0, 0, NB)
         gather(9, 1)
+        interleave(vcopy, 2, 0, NB, HALF)
         gather(10, 1)
-        quantize(2, 0)
+        quantize(2, 0, HALF)
         multiply(2, 0)
+        multiply(0, 1, (1,))
+        multiply(1, 1, (1,))
         gather(11, 1)
         gelu(0, 0)
-        interleave(nc.vector.tensor_copy, 2, 1)
         gelu(1, 0)
         scatter(0, 0)
-        quantize(2, 1)
+        interleave(scopy, 2, 1)
+        quantize(2, HALF, S)
         multiply(2, 1)
         gelu(0, 1)
         gelu(1, 1)

@@ -34,7 +34,7 @@ def tile_list_hboth_gelu_kernel(tc, xT, w4_words, w4_scales, r8_words, r8_scales
         offs2_sb = keep.tile([P, S // 16], U16, name="offs2_sb")
         x = [keep.tile([P, T], F32, name="x%d" % i) for i in range(4 * PASSES)]
         wgt_sb = [keep.tile([P, HALF], F32, name="wgt%d" % s) for s in range(2)]
-        wgo_sb = keep.tile([P, S], F32, name="wgo_sb")
+        wgo_sb = [keep.tile([P, HALF], F32, name="wgo%d" % s) for s in range(2)]
         b_sb = keep.tile([P, 2], F32, name="b_sb")
         w4 = keep.tile([P, PASSES, 2 * M], U8, name="w4", align_bytes=64)
         r8 = keep.tile([P, PASSES, 4 * M], U8, name="r8", align_bytes=64)
@@ -74,7 +74,8 @@ def tile_list_hboth_gelu_kernel(tc, xT, w4_words, w4_scales, r8_words, r8_scales
         with nc.allow_non_contiguous_dma(reason="one bias value a partition"):
             nc.sync.dma_start(b_sb[:], b.rearrange("(m p) -> p m", p=P))
         nc.sync.dma_start(offs2_sb[:], offs2)
-        nc.sync.dma_start(wgo_sb[:], wgo)
+        for s in range(2):
+            nc.sync.dma_start(wgo_sb[s][:], wgo[:, s * HALF : (s + 1) * HALF])
 
         g4, grouped, codes, scales_x = {}, {}, {}, {}
         for a in range(PASSES):
@@ -104,8 +105,8 @@ def tile_list_hboth_gelu_kernel(tc, xT, w4_words, w4_scales, r8_words, r8_scales
 
         def interleave(eng, a, s, lo=0, hi=HALF):
             eng(
-                grouped[a][:, s * HALF + lo : s * HALF + hi, :],
-                g4[a, s][:, :, lo:hi].rearrange("p t n -> p n t"),
+                grouped[a][:, s * HALF + lo : s * HALF + hi, :].rearrange("p (c i) t -> p c t i", i=4),
+                g4[a, s][:, :, lo:hi].rearrange("p t (c i) -> p c t i", i=4),
             )
 
         def quantize(a, lo, hi):
@@ -115,8 +116,8 @@ def tile_list_hboth_gelu_kernel(tc, xT, w4_words, w4_scales, r8_words, r8_scales
                 in_=grouped[a][:, lo:hi, :].rearrange("p n t -> p (n t)"),
             )
 
-        def multiply(a, s, formats=(0, 1)):
-            for m in range(2):
+        def multiply(a, s, formats=(0, 1), blocks=(0, 1)):
+            for m in blocks:
                 for c in range(2):
                     cols = slice(s * HALF + c * NB, s * HALF + (c + 1) * NB)
                     for f in formats:
@@ -144,7 +145,7 @@ def tile_list_hboth_gelu_kernel(tc, xT, w4_words, w4_scales, r8_words, r8_scales
             nc.vector.tensor_tensor(
                 win[m][:].indirect(offs2_sb[:, s * LCOLS : (s + 1) * LCOLS]),
                 gel[m, s][:],
-                wgo_sb[:, s * HALF : (s + 1) * HALF],
+                wgo_sb[s][:],
                 MULT,
             )
 
@@ -171,22 +172,26 @@ def tile_list_hboth_gelu_kernel(tc, xT, w4_words, w4_scales, r8_words, r8_scales
         quantize(1, 0, S)
         multiply(1, 0, (0,))
         multiply(1, 1, (0,))
-        multiply(0, 0, (1,))
-        multiply(1, 0, (1,))
+        multiply(0, 0, (1,), (0,))
+        multiply(1, 0, (1,), (0,))
         gather(11, 0)
         interleave(scopy, 2, 0, 0, NB)
         gather(9, 1)
         interleave(vcopy, 2, 0, NB, HALF)
         gather(10, 1)
         quantize(2, 0, HALF)
-        multiply(2, 0)
+        multiply(2, 0, (0, 1), (0,))
+        multiply(0, 0, (1,), (1,))
+        multiply(1, 0, (1,), (1,))
+        multiply(2, 0, (0, 1), (1,))
         multiply(0, 1, (1,))
         multiply(1, 1, (1,))
         gather(11, 1)
+        interleave(vcopy, 2, 1, NB, HALF)
         gelu(0, 0)
         gelu(1, 0)
         scatter(0, 0)
-        interleave(scopy, 2, 1)
+        interleave(scopy, 2, 1, 0, NB)
         quantize(2, HALF, S)
         multiply(2, 1)
         gelu(0, 1)

@@ -66,9 +66,9 @@ def tile_list_hboth_gelu_kernel(tc, xT, w4_words, w4_scales, r8_words, r8_scales
 
         for i in range(1, 10):
             load_x(i)
-        nc.sync.dma_start(w4[:].bitcast(I32), w4_words.rearrange("a p b -> p a b").bitcast(I32))
         load_x(10)
         load_x(11)
+        nc.sync.dma_start(w4[:].bitcast(I32), w4_words.rearrange("a p b -> p a b").bitcast(I32))
         r8_view = r8_words.rearrange("a p n i -> p a (n i)").bitcast(I32)
         nc.sync.dma_start(r8[:].bitcast(I32), r8_view)
         with nc.allow_non_contiguous_dma(reason="one bias value a partition"):
@@ -159,8 +159,6 @@ def tile_list_hboth_gelu_kernel(tc, xT, w4_words, w4_scales, r8_words, r8_scales
             gather(i, 0)
             gather(i, 1)
         quantize(0, 0, S)
-        multiply(0, 0, (0,))
-        multiply(0, 1, (0,))
         gather(7, 0)
         gather(7, 1)
         interleave(scopy, 1, 0)
@@ -170,22 +168,23 @@ def tile_list_hboth_gelu_kernel(tc, xT, w4_words, w4_scales, r8_words, r8_scales
         gather(9, 0)
         gather(10, 0)
         quantize(1, 0, S)
+        multiply(0, 0, (0,))
         multiply(1, 0, (0,))
-        multiply(1, 1, (0,))
         multiply(0, 0, (1,), (0,))
         multiply(1, 0, (1,), (0,))
         gather(11, 0)
         interleave(scopy, 2, 0, 0, NB)
         gather(9, 1)
         interleave(vcopy, 2, 0, NB, HALF)
+        quantize(2, 0, NB)
+        quantize(2, NB, HALF)
         gather(10, 1)
-        quantize(2, 0, HALF)
         multiply(2, 0, (0, 1), (0,))
         multiply(0, 0, (1,), (1,))
         multiply(1, 0, (1,), (1,))
         multiply(2, 0, (0, 1), (1,))
-        multiply(0, 1, (1,))
-        multiply(1, 1, (1,))
+        multiply(0, 1)
+        multiply(1, 1)
         gather(11, 1)
         interleave(vcopy, 2, 1, NB, HALF)
         gelu(0, 0)

from contextlib import ExitStack

import concourse.mybir as mybir

K, M, T, S = 1536, 256, 1024, 512

F32 = mybir.dt.float32
BF16 = mybir.dt.bfloat16
I32 = mybir.dt.int32
U32 = mybir.dt.uint32
U16 = mybir.dt.uint16
U8 = mybir.dt.uint8
FP8X4 = mybir.dt.float8_e4m3fn_x4
FP4X4 = mybir.dt.float4_e2m1fn_x4
MULT = mybir.AluOpType.mult
GELU = mybir.ActivationFunctionType.Gelu_apprx_tanh

P = 128
PASSES = K // 512
HALF = S // 2
LCOLS = HALF // 16
NB = 128

FLOPS = 2 * 2 * K * M * S


def tile_list_hboth_gelu_kernel(tc, xT, w4_words, w4_scales, r8_words, r8_scales, wgt, b, wgo, offs, offs2, out):
    nc = tc.nc
    with ExitStack() as ctx:
        keep = ctx.enter_context(tc.tile_pool(name="keep", bufs=1))
        psum = ctx.enter_context(tc.psum_pool(name="psum", bufs=1))

        offs_sb = keep.tile([P, S // 16], U16, name="offs_sb")
        offs2_sb = keep.tile([P, S // 16], U16, name="offs2_sb")
        x = [keep.tile([P, T], F32, name="x%d" % i) for i in range(4 * PASSES)]
        wgt_sb = [keep.tile([P, HALF], F32, name="wgt%d" % s) for s in range(2)]
        wgo_sb = [keep.tile([P, HALF], F32, name="wgo%d" % s) for s in range(2)]
        b_sb = keep.tile([P, 2], F32, name="b_sb")
        w4 = keep.tile([P, PASSES, 2 * M], U8, name="w4", align_bytes=64)
        r8 = keep.tile([P, PASSES, 4 * M], U8, name="r8", align_bytes=64)
        ws = keep.tile([P, 2, PASSES, M], U8, name="ws", align_bytes=64)
        win = [keep.tile([P, T], F32, name="win%d" % m) for m in range(2)]
        warm = keep.tile([P, 1], F32, name="warm")

        nc.sync.dma_start(offs_sb[:], offs)
        x_view = xT.rearrange("(a p i) t -> a i p t", p=P, i=4)

        def load_x(i):
            nc.sync.dma_start(x[i][:], x_view[i // 4, i % 4])

        load_x(0)
        nc.scalar.dma_start(wgt_sb[0][:], wgt[:, 0:HALF])
        nc.sync.dma_start(wgt_sb[1][:], wgt[:, HALF:S])

        nc.vector.memset(ws[:].rearrange("p f a m -> p (f a m)").bitcast(I32), 0)
        for f, scales in enumerate((w4_scales, r8_scales)):
            for q in range(4):
                nc.gpsimd.dma_start(
                    ws[32 * q : 32 * q + 4, f, :, :].bitcast(I32),
                    scales[:, 4 * q : 4 * q + 4, :].rearrange("a q m -> q a m").bitcast(I32),
                )
        nc.vector.memset(warm[:], 0.0)
        nc.scalar.activation(warm[:], warm[:], GELU)
        for m in range(2):
            nc.vector.memset(win[m][:], 0.0)

        for i in range(1, 10):
            load_x(i)
        load_x(10)
        load_x(11)
        nc.sync.dma_start(w4[:].bitcast(I32), w4_words.rearrange("a p b -> p a b").bitcast(I32))
        r8_view = r8_words.rearrange("a p n i -> p a (n i)").bitcast(I32)
        nc.sync.dma_start(r8[:].bitcast(I32), r8_view)
        with nc.allow_non_contiguous_dma(reason="one bias value a partition"):
            nc.sync.dma_start(b_sb[:], b.rearrange("(m p) -> p m", p=P))
        nc.sync.dma_start(offs2_sb[:], offs2)
        for s in range(2):
            nc.sync.dma_start(wgo_sb[s][:], wgo[:, s * HALF : (s + 1) * HALF])

        g4, grouped, codes, scales_x = {}, {}, {}, {}
        for a in range(PASSES):
            grouped[a] = keep.tile([P, S, 4], BF16, name="gr%d" % a, align_bytes=64)
            codes[a] = keep.tile([P, S], U32, name="co%d" % a, align_bytes=64)
            scales_x[a] = keep.tile([P, S], U8, name="sc%d" % a, align_bytes=64)
            for s in range(2):
                k = "_%d%d" % (a, s)
                g4[a, s] = keep.tile([P, 4, HALF], F32, name="g4" + k)
        acc = {}
        for m in range(2):
            for s in range(2):
                for c in range(2):
                    acc[m, s, c] = psum.tile([P, 512], F32, name="acc%d%d%d" % (m, s, c))
        gel = {}
        for m in range(2):
            for s in range(2):
                gel[m, s] = keep.tile([P, HALF], F32, name="gel%d%d" % (m, s))

        def gather(i, s):
            nc.vector.tensor_tensor(
                g4[i // 4, s][:, i % 4, :],
                x[i][:].indirect(offs_sb[:, s * LCOLS : (s + 1) * LCOLS]),
                wgt_sb[s][:],
                MULT,
            )

        def interleave(eng, a, s, lo=0, hi=HALF):
            eng(
                grouped[a][:, s * HALF + lo : s * HALF + hi, :].rearrange("p (c i) t -> p c t i", i=4),
                g4[a, s][:, :, lo:hi].rearrange("p t (c i) -> p c t i", i=4),
            )

        def quantize(a, lo, hi):
            nc.vector.quantize_mx(
                out=codes[a][:, lo:hi].bitcast(FP8X4),
                scales=scales_x[a][:, lo:hi],
                in_=grouped[a][:, lo:hi, :].rearrange("p n t -> p (n t)"),
            )

        def multiply(a, s, formats=(0, 1), blocks=(0, 1)):
            for m in blocks:
                for c in range(2):
                    cols = slice(s * HALF + c * NB, s * HALF + (c + 1) * NB)
                    for f in formats:
                        if f == 0:
                            w = w4[:, a, 256 * m : 256 * m + 256].bitcast(FP4X4)
                        else:
                            w = r8[:, a, 512 * m : 512 * m + 512].bitcast(FP8X4)
                        nc.tensor.matmul_mx(
                            out=acc[m, s, c][:, 0:NB],
                            lhsT=w,
                            lhsT_scale=ws[:, f, a, 128 * m : 128 * m + 128],
                            rhs=codes[a][:, cols].bitcast(FP8X4),
                            rhs_scale=scales_x[a][:, cols],
                            start=(a == 0 and f == 0),
                            stop=(a == PASSES - 1 and f == 1),
                        )

        def gelu(m, s):
            for c in range(2):
                nc.scalar.activation(
                    gel[m, s][:, c * NB : (c + 1) * NB], acc[m, s, c][:, 0:NB], GELU, bias=b_sb[:, m : m + 1]
                )

        def scatter(m, s):
            nc.vector.tensor_tensor(
                win[m][:].indirect(offs2_sb[:, s * LCOLS : (s + 1) * LCOLS]),
                gel[m, s][:],
                wgo_sb[s][:],
                MULT,
            )

        scopy, vcopy = nc.scalar.copy, nc.vector.tensor_copy
        for i in range(4):
            gather(i, 0)
            gather(i, 1)
        interleave(scopy, 0, 0)
        interleave(scopy, 0, 1)
        for i in range(4, 7):
            gather(i, 0)
            gather(i, 1)
        quantize(0, 0, S)
        gather(7, 0)
        gather(7, 1)
        interleave(scopy, 1, 0)
        interleave(scopy, 1, 1)
        gather(8, 0)
        gather(8, 1)
        gather(9, 0)
        gather(10, 0)
        quantize(1, 0, S)
        multiply(0, 0, (0,))
        multiply(1, 0, (0,))
        multiply(0, 0, (1,), (0,))
        multiply(1, 0, (1,), (0,))
        gather(11, 0)
        interleave(scopy, 2, 0, 0, NB)
        gather(9, 1)
        interleave(vcopy, 2, 0, NB, HALF)
        quantize(2, 0, NB)
        quantize(2, NB, HALF)
        gather(10, 1)
        multiply(2, 0, (0, 1), (0,))
        multiply(0, 0, (1,), (1,))
        multiply(1, 0, (1,), (1,))
        multiply(2, 0, (0, 1), (1,))
        multiply(0, 1)
        multiply(1, 1)
        gather(11, 1)
        interleave(vcopy, 2, 1, NB, HALF)
        gelu(0, 0)
        gelu(1, 0)
        scatter(0, 0)
        interleave(scopy, 2, 1, 0, NB)
        quantize(2, HALF, S)
        multiply(2, 1)
        gelu(0, 1)
        gelu(1, 1)
        scatter(1, 0)
        scatter(0, 1)
        nc.sync.dma_start(out[0:P, :], win[0][:])
        scatter(1, 1)
        nc.sync.dma_start(out[P : 2 * P, :], win[1][:])
